import numpy as np
CORES = [24,26,29,31,48,50,53,55]
N = 8
TK = 512
D = 128 * N
EPS = 0.01
def setup_inputs(rng):
    return {"x": (rng.standard_normal((N, 128, TK), dtype=np.float32) * (0.5 + np.abs(rng.standard_normal((1, 1, TK), dtype=np.float32))) + rng.standard_normal((1, 1, TK), dtype=np.float32))}
def setup_inputs_big(rng):
    d = setup_inputs(rng)
    for k in ("x",): d[k] = (d[k].astype(np.float32) * 1024.0).astype(d[k].dtype)
    return d
def setup_inputs_small(rng):
    d = setup_inputs(rng)
    for k in ("x",): d[k] = (d[k].astype(np.float32) * (1 / 1024.0)).astype(d[k].dtype)
    return d
def setup_inputs_apart(rng):
    d = setup_inputs(rng)
    f = (10.0 ** rng.permutation(np.linspace(-1.5, 1.5, N))).astype(np.float32).reshape(N, 1, 1)
    for k in ("x",): d[k] = (d[k].astype(np.float32) * f).astype(d[k].dtype)
    return d
def setup_inputs_mixed(rng):
    d = setup_inputs(rng)
    f = (10.0 ** rng.uniform(-3, 3, (1, 1, TK))).astype(np.float32); shape = rng.integers(3, size=(1, 1, TK))
    for k in ("x",):
        x = d[k].astype(np.float32)
        m = x.mean(axis=(0, 1), keepdims=True); level = m + np.sign(x - m) * np.abs(x - m).mean(axis=(0, 1), keepdims=True) * rng.uniform(0.9, 1.1, x.shape).astype(np.float32)
        other = x * np.where(rng.random(x.shape) < 0.5, 0.1, 1.0).astype(np.float32)
        d[k] = (np.where(shape == 1, level, np.where(shape == 2, other, x)) * f).astype(d[k].dtype)
    return d
def setup_inputs_offset(rng):
    d = setup_inputs(rng)
    x = d["x"]; spread = x.std(axis=(0, 1), keepdims=True)
    d["x"] = (x + spread * rng.uniform(16, 48, (1, 1, TK)) * rng.choice([-1.0, 1.0], (1, 1, TK))).astype(np.float32)
    return d
def reference(x):
    X = x.astype(np.float64)
    mu = X.sum(axis=(0, 1)) / D
    Z = X - mu
    Z = Z / np.sqrt((Z ** 2).sum(axis=(0, 1)) / D + EPS)
    return {"y": Z.astype(np.float32)}

@@ -1,0 +1,195 @@
+import numpy as np
+from concourse.bass import DstId, RemoteDMATransfer
+from concourse.mybir import dt, AluOpType, AxisListType, ActivationFunctionType
+
+P = 128
+NR = 8
+EPS = 0.01
+PARTS = ((0, 2), (2, 4))
+
+
+def _width(nb):
+    return ((2 * nb + 3) // 4) * 4
+
+
+SCRATCH = {
+    "xs": ("sbuf", [P, 512], "float32"),
+    "ones": ("sbuf", [P, P], "float32"),
+    "idx": ("sbuf", [P, 132], "float32"),
+    "junk": ("sbuf", [P, 512], "float32"),
+    "yT": ("sbuf", [P, 512], "float32"),
+    "ys": ("sbuf", [P, 512], "float32"),
+}
+SEMAPHORES = ["c1", "c2", "sent"]
+for _b in range(4):
+    SCRATCH["xT%d" % _b] = ("psum", [P, 512], "float32")
+    SCRATCH["yo%d" % _b] = ("psum", [P, 512], "float32")
+    SEMAPHORES += [n + str(_b) for n in ("tr", "ucp", "sq", "ap", "bt", "cp", "st")]
+for _p, (_lo, _hi) in enumerate(PARTS):
+    _nb = _hi - _lo
+    SCRATCH["G%d" % _p] = ("sbuf", [P, NR * _width(_nb)], "float32")
+    SCRATCH["js%d" % _p] = ("sbuf", [P, 2 * _nb * NR], "float32")
+    for _n in ("nU", "E", "SQ", "w", "v", "sd", "r", "mu"):
+        SCRATCH["%s%d" % (_n, _p)] = ("sbuf", [P, _nb], "float32")
+    SEMAPHORES += [n + str(_p) for n in ("ld", "pad", "on", "off", "snu", "se", "ssq", "sw", "smu", "sv", "ssd", "sr")]
+
+
+def _bits(mask):
+    return [e for e in range(mask.bit_length()) if (mask >> e) & 1]
+
+
+def _mask(engines):
+    return sum(1 << e for e in engines)
+
+
+def _pow2(n):
+    k = 1
+    while k * 2 <= n:
+        k *= 2
+    return k
+
+
+def _plan(cores, topo):
+    order = sorted(cores, key=lambda c: (topo.chip(c), cores.index(c)))
+    slot = {c: i for i, c in enumerate(order)}
+    on, off = {}, {}
+    for c in cores:
+        here = [d for d in cores if topo.chip(d) == topo.chip(c)]
+        there = [d for d in cores if topo.chip(d) != topo.chip(c)]
+        relays = [d for d in here if all(topo.may_write(d, e) for e in there)]
+        peers = [d for d in here if d != c]
+        far = _bits(topo.mask(c, there[0]))
+        near = [e for e in _bits(topo.mask(c, peers[0])) if e not in far]
+        urgent = [d for d in peers if d in relays]
+        rest = [d for d in peers if d not in relays]
+        k = _pow2(len(far) // max(1, len(urgent)))
+        tr = [([d], far[i * k:(i + 1) * k]) for i, d in enumerate(urgent)]
+        if rest:
+            tr.append((rest, near[:_pow2(len(near))]))
+        on[c] = tr
+        if c in relays:
+            mine = []
+            for i, d in enumerate(there):
+                same = [r for r in relays if topo.die(r) == topo.die(d)]
+                if (same[0] if same else relays[i % len(relays)]) == c:
+                    mine.append(d)
+            k = _pow2(len(far) // max(1, len(mine)))
+            off[c] = [([d], far[i * k:(i + 1) * k]) for i, d in enumerate(mine)]
+    return slot, on, off
+
+
+def rank_program(g, core, T, topo):
+    if T.rank_of(core) is None:
+        return
+    S = T.sem
+    ACT = ActivationFunctionType
+    ALU = AluOpType
+    cores = list(T.cores)
+    slot, on, off = _plan(cores, topo)
+    me = slot[core]
+    here = sorted(slot[d] for d in cores if topo.chip(d) == topo.chip(core))
+    n_on = sum(len(e) for c in cores if c != core for ds, e in on[c] if core in ds)
+    n_off = sum(len(e) for c in off for ds, e in off[c] if core in ds)
+    ident = T.idx[:, 0:P]
+
+    def blk(b):
+        return slice(b * P, (b + 1) * P)
+
+    def send(transfers, piece, sem):
+        g.remote_dma_fused(
+            [RemoteDMATransfer(dst_ids=[DstId(rid=topo.addr(d)[0], pnc=topo.addr(d)[1]) for d in ds],
+                               dma_engine_mask=_mask(e), remote_sem=sem, srcs=[piece], dsts=[piece for d in ds])
+             for ds, e in transfers], local_sem=S.sent)
+        return sum(len(e) for ds, e in transfers)
+
+    for p, (lo, hi) in enumerate(PARTS):
+        q = g.sync if p % 2 == 0 else g.scalar
+        q.dma_start(T.xs[:, lo * P:hi * P], T.x[:, lo * P:hi * P]).then_inc(S["ld%d" % p], 16)
+    g.vector.memset(T.ones[:], 1.0).then_inc(S.c1, 1)
+    g.vector.memset(T.idx[:, P:P + 1], -1.0 / 4096.0).then_inc(S.c2, 1)
+    g.wait_ge(S.c1, 1)
+    g.affine_select(ident, T.ones[:], [[-1, P]], ALU.is_equal, 0.0, 0, 1).then_inc(S.c2, 1)
+    for p, (lo, hi) in enumerate(PARTS):
+        nb, W = hi - lo, _width(hi - lo)
+        if W > 2 * nb:
+            g.vector.memset(T["G%d" % p][:, me * W + 2 * nb:(me + 1) * W], 0.0).then_inc(S["pad%d" % p], 1)
+
+    g.tensor.wait_ge(S.c2, 2)
+    for p, (lo, hi) in enumerate(PARTS):
+        nb, W, G = hi - lo, _width(hi - lo), T["G%d" % p]
+        g.tensor.wait_ge(S["ld%d" % p], 16)
+        for b in range(lo, hi):
+            j = b - lo
+            xT = T["xT%d" % b]
+            ucol = G[:, me * W + j:me * W + j + 1]
+            g.tensor.matmul(xT[:, 0:P + 1], T.xs[:, blk(b)], T.idx[:, 0:P + 1], True, True).then_inc(S["tr%d" % b], 1)
+            g.vector.wait_ge(S["tr%d" % b], 1)
+            g.vector.tensor_copy(ucol, xT[:, P:P + 1]).then_inc(S["ucp%d" % b], 1)
+            g.scalar.wait_ge(S["tr%d" % b], 1)
+            g.scalar.wait_ge(S["ucp%d" % b], 1)
+            g.scalar.activation(T.junk[:, blk(b)], xT[:, 0:P], ACT.Square, bias=ucol, scale=1.0 / 32.0,
+                                accum_out=G[:, me * W + nb + j:me * W + nb + j + 1]).then_inc(S["sq%d" % b], 1)
+
+    sent = 0
+    for p, (lo, hi) in enumerate(PARTS):
+        nb, W, G = hi - lo, _width(hi - lo), T["G%d" % p]
+        if W > 2 * nb:
+            g.wait_ge(S["pad%d" % p], 1)
+        for b in range(lo, hi):
+            g.wait_ge(S["ucp%d" % b], 1)
+            g.wait_ge(S["sq%d" % b], 1)
+        sent += send(on[core], G[:, me * W:(me + 1) * W], S["on%d" % p])
+    if core in off:
+        for p, (lo, hi) in enumerate(PARTS):
+            W, G = _width(hi - lo), T["G%d" % p]
+            g.wait_ge(S["on%d" % p], n_on)
+            sent += send(off[core], G[:, here[0] * W:(here[-1] + 1) * W], S["off%d" % p])
+    g.wait_ge(S.sent, sent)
+
+    V, A = g.vector, g.scalar
+    for p, (lo, hi) in enumerate(PARTS):
+        nb, W, G, js = hi - lo, _width(hi - lo), T["G%d" % p], T["js%d" % p]
+        t = lambda n: T["%s%d" % (n, p)]
+        s = lambda n: S["%s%d" % (n, p)]
+        for q in (V, A):
+            q.wait_ge(s("on"), n_on)
+            q.wait_ge(s("off"), n_off)
+            for b in range(lo, hi):
+                q.wait_ge(S["ucp%d" % b], 1)
+                q.wait_ge(S["sq%d" % b], 1)
+        for j in range(nb):
+            A.activation(js[:, j * NR:(j + 1) * NR], G[:, j:NR * W:W], ACT.Copy, scale=-1.0 / NR,
+                         accum_out=t("nU")[:, j:j + 1]).then_inc(s("snu"), 1)
+        A.wait_ge(s("snu"), nb)
+        for j in range(nb):
+            A.activation(js[:, (nb + j) * NR:(nb + j + 1) * NR], G[:, j:NR * W:W], ACT.Square,
+                         bias=t("nU")[:, j:j + 1], accum_out=t("E")[:, j:j + 1]).then_inc(s("se"), 1)
+        for j in range(nb):
+            V.tensor_reduce(t("SQ")[:, j:j + 1], G[:, nb + j:NR * W:W], AxisListType.X, ALU.add).then_inc(s("ssq"), 1)
+        V.wait_ge(s("ssq"), nb)
+        V.tensor_scalar(t("w")[:], t("SQ")[:], EPS, 1.0 / 128.0, ALU.add, ALU.mult).then_inc(s("sw"), 1)
+        V.wait_ge(s("snu"), nb)
+        V.tensor_scalar(t("mu")[:], t("nU")[:], 32.0, None, ALU.mult).then_inc(s("smu"), 1)
+        V.wait_ge(s("se"), nb)
+        V.wait_ge(s("sw"), 1)
+        V.tensor_tensor(t("v")[:], t("E")[:], t("w")[:], ALU.add).then_inc(s("sv"), 1)
+        A.wait_ge(s("sv"), 1)
+        A.activation(t("sd")[:], t("v")[:], ACT.Sqrt, scale=128.0).then_inc(s("ssd"), 1)
+        V.wait_ge(s("ssd"), 1)
+        V.reciprocal(t("r")[:], t("sd")[:]).then_inc(s("sr"), 1)
+        V.wait_ge(s("sr"), 1)
+        V.wait_ge(s("smu"), 1)
+        for b in range(lo, hi):
+            j = b - lo
+            V.tensor_scalar(T.yT[:, blk(b)], T["xT%d" % b][:, 0:P], t("mu")[:, j:j + 1], t("r")[:, j:j + 1],
+                            ALU.subtract, ALU.mult).then_inc(S["ap%d" % b], 1)
+            g.tensor.wait_ge(S["ap%d" % b], 1)
+            g.tensor.matmul(T["yo%d" % b][:, 0:P], T.yT[:, blk(b)], ident, True, True).then_inc(S["bt%d" % b], 1)
+
+    for b in range(4):
+        A.wait_ge(S["bt%d" % b], 1)
+        A.activation(T.ys[:, blk(b)], T["yo%d" % b][:, 0:P], ACT.Copy).then_inc(S["cp%d" % b], 1)
+        g.sync.wait_ge(S["cp%d" % b], 1)
+        g.sync.dma_start(T.y[:, blk(b)], T.ys[:, blk(b)]).then_inc(S["st%d" % b], 16)
+    for b in range(4):
+        g.sync.wait_ge(S["st%d" % b], 16)

@@ -5,7 +5,7 @@ from concourse.mybir import dt, AluOpType, AxisListType, ActivationFunctionType
 P = 128
 NR = 8
 EPS = 0.01
-PARTS = ((0, 2), (2, 4))
+PARTS = ((0, 1), (1, 4))
 
 
 def _width(nb):
@@ -24,14 +24,14 @@ SEMAPHORES = ["c1", "c2", "sent"]
 for _b in range(4):
     SCRATCH["xT%d" % _b] = ("psum", [P, 512], "float32")
     SCRATCH["yo%d" % _b] = ("psum", [P, 512], "float32")
-    SEMAPHORES += [n + str(_b) for n in ("tr", "ucp", "sq", "ap", "bt", "cp", "st")]
+    SEMAPHORES += [n + str(_b) for n in ("ld", "tr", "ucp", "sq", "ap", "bt", "cp", "st")]
 for _p, (_lo, _hi) in enumerate(PARTS):
     _nb = _hi - _lo
     SCRATCH["G%d" % _p] = ("sbuf", [P, NR * _width(_nb)], "float32")
-    SCRATCH["js%d" % _p] = ("sbuf", [P, 2 * _nb * NR], "float32")
-    for _n in ("nU", "E", "SQ", "w", "v", "sd", "r", "mu"):
+    SCRATCH["js%d" % _p] = ("sbuf", [P, _nb * NR], "float32")
+    for _n in ("NS", "E", "SQ", "w", "v", "sd", "r", "mu"):
         SCRATCH["%s%d" % (_n, _p)] = ("sbuf", [P, _nb], "float32")
-    SEMAPHORES += [n + str(_p) for n in ("ld", "pad", "on", "off", "snu", "se", "ssq", "sw", "smu", "sv", "ssd", "sr")]
+    SEMAPHORES += [n + str(_p) for n in ("pad", "on", "off", "sns", "se", "ssq", "sw", "smu", "sv", "ssd", "sr")]
 
 
 def _bits(mask):
@@ -63,10 +63,9 @@ def _plan(cores, topo):
         urgent = [d for d in peers if d in relays]
         rest = [d for d in peers if d not in relays]
         k = _pow2(len(far) // max(1, len(urgent)))
-        tr = [([d], far[i * k:(i + 1) * k]) for i, d in enumerate(urgent)]
+        on[c] = [[([d], far[i * k:(i + 1) * k]) for i, d in enumerate(urgent)]]
         if rest:
-            tr.append((rest, near[:_pow2(len(near))]))
-        on[c] = tr
+            on[c].append([(rest, near[:_pow2(len(near))])])
         if c in relays:
             mine = []
             for i, d in enumerate(there):
@@ -84,13 +83,15 @@ def rank_program(g, core, T, topo):
     S = T.sem
     ACT = ActivationFunctionType
     ALU = AluOpType
+    V, A = g.vector, g.scalar
     cores = list(T.cores)
     slot, on, off = _plan(cores, topo)
     me = slot[core]
     here = sorted(slot[d] for d in cores if topo.chip(d) == topo.chip(core))
-    n_on = sum(len(e) for c in cores if c != core for ds, e in on[c] if core in ds)
+    n_on = sum(len(e) for c in cores if c != core for call in on[c] for ds, e in call if core in ds)
     n_off = sum(len(e) for c in off for ds, e in off[c] if core in ds)
     ident = T.idx[:, 0:P]
+    NP = len(PARTS)
 
     def blk(b):
         return slice(b * P, (b + 1) * P)
@@ -102,33 +103,33 @@ def rank_program(g, core, T, topo):
              for ds, e in transfers], local_sem=S.sent)
         return sum(len(e) for ds, e in transfers)
 
-    for p, (lo, hi) in enumerate(PARTS):
-        q = g.sync if p % 2 == 0 else g.scalar
-        q.dma_start(T.xs[:, lo * P:hi * P], T.x[:, lo * P:hi * P]).then_inc(S["ld%d" % p], 16)
-    g.vector.memset(T.ones[:], 1.0).then_inc(S.c1, 1)
-    g.vector.memset(T.idx[:, P:P + 1], -1.0 / 4096.0).then_inc(S.c2, 1)
+    for b in range(4):
+        q = g.sync if b % 2 == 0 else g.scalar
+        q.dma_start(T.xs[:, blk(b)], T.x[:, blk(b)]).then_inc(S["ld%d" % b], 16)
+    V.memset(T.ones[:], 1.0).then_inc(S.c1, 1)
+    V.memset(T.idx[:, P:P + 1], -1.0 / 32768.0).then_inc(S.c2, 1)
     g.wait_ge(S.c1, 1)
     g.affine_select(ident, T.ones[:], [[-1, P]], ALU.is_equal, 0.0, 0, 1).then_inc(S.c2, 1)
     for p, (lo, hi) in enumerate(PARTS):
         nb, W = hi - lo, _width(hi - lo)
         if W > 2 * nb:
-            g.vector.memset(T["G%d" % p][:, me * W + 2 * nb:(me + 1) * W], 0.0).then_inc(S["pad%d" % p], 1)
+            V.memset(T["G%d" % p][:, me * W + 2 * nb:(me + 1) * W], 0.0).then_inc(S["pad%d" % p], 1)
 
     g.tensor.wait_ge(S.c2, 2)
     for p, (lo, hi) in enumerate(PARTS):
         nb, W, G = hi - lo, _width(hi - lo), T["G%d" % p]
-        g.tensor.wait_ge(S["ld%d" % p], 16)
         for b in range(lo, hi):
             j = b - lo
             xT = T["xT%d" % b]
             ucol = G[:, me * W + j:me * W + j + 1]
+            g.tensor.wait_ge(S["ld%d" % b], 16)
             g.tensor.matmul(xT[:, 0:P + 1], T.xs[:, blk(b)], T.idx[:, 0:P + 1], True, True).then_inc(S["tr%d" % b], 1)
-            g.vector.wait_ge(S["tr%d" % b], 1)
-            g.vector.tensor_copy(ucol, xT[:, P:P + 1]).then_inc(S["ucp%d" % b], 1)
-            g.scalar.wait_ge(S["tr%d" % b], 1)
-            g.scalar.wait_ge(S["ucp%d" % b], 1)
-            g.scalar.activation(T.junk[:, blk(b)], xT[:, 0:P], ACT.Square, bias=ucol, scale=1.0 / 32.0,
-                                accum_out=G[:, me * W + nb + j:me * W + nb + j + 1]).then_inc(S["sq%d" % b], 1)
+            V.wait_ge(S["tr%d" % b], 1)
+            V.tensor_copy(ucol, xT[:, P:P + 1]).then_inc(S["ucp%d" % b], 1)
+            A.wait_ge(S["tr%d" % b], 1)
+            A.wait_ge(S["ucp%d" % b], 1)
+            A.activation(T.junk[:, blk(b)], xT[:, 0:P], ACT.Square, bias=ucol, scale=1.0 / 256.0,
+                         accum_out=G[:, me * W + nb + j:me * W + nb + j + 1]).then_inc(S["sq%d" % b], 1)
 
     sent = 0
     for p, (lo, hi) in enumerate(PARTS):
@@ -138,7 +139,8 @@ def rank_program(g, core, T, topo):
         for b in range(lo, hi):
             g.wait_ge(S["ucp%d" % b], 1)
             g.wait_ge(S["sq%d" % b], 1)
-        sent += send(on[core], G[:, me * W:(me + 1) * W], S["on%d" % p])
+        for call in on[core]:
+            sent += send(call, G[:, me * W:(me + 1) * W], S["on%d" % p])
     if core in off:
         for p, (lo, hi) in enumerate(PARTS):
             W, G = _width(hi - lo), T["G%d" % p]
@@ -146,35 +148,40 @@ def rank_program(g, core, T, topo):
             sent += send(off[core], G[:, here[0] * W:(here[-1] + 1) * W], S["off%d" % p])
     g.wait_ge(S.sent, sent)
 
-    V, A = g.vector, g.scalar
-    for p, (lo, hi) in enumerate(PARTS):
-        nb, W, G, js = hi - lo, _width(hi - lo), T["G%d" % p], T["js%d" % p]
-        t = lambda n: T["%s%d" % (n, p)]
-        s = lambda n: S["%s%d" % (n, p)]
-        for q in (V, A):
-            q.wait_ge(s("on"), n_on)
-            q.wait_ge(s("off"), n_off)
-            for b in range(lo, hi):
-                q.wait_ge(S["ucp%d" % b], 1)
-                q.wait_ge(S["sq%d" % b], 1)
+    def names(p):
+        lo, hi = PARTS[p]
+        return (lo, hi, hi - lo, _width(hi - lo), T["G%d" % p],
+                lambda n: T["%s%d" % (n, p)], lambda n: S["%s%d" % (n, p)])
+
+    def arrived(q, p):
+        lo, hi, nb, W, G, t, s = names(p)
+        q.wait_ge(s("on"), n_on)
+        q.wait_ge(s("off"), n_off)
+        for b in range(lo, hi):
+            q.wait_ge(S["ucp%d" % b], 1)
+            q.wait_ge(S["sq%d" % b], 1)
+
+    def prep(p):
+        lo, hi, nb, W, G, t, s = names(p)
+        arrived(V, p)
         for j in range(nb):
-            A.activation(js[:, j * NR:(j + 1) * NR], G[:, j:NR * W:W], ACT.Copy, scale=-1.0 / NR,
-                         accum_out=t("nU")[:, j:j + 1]).then_inc(s("snu"), 1)
-        A.wait_ge(s("snu"), nb)
-        for j in range(nb):
-            A.activation(js[:, (nb + j) * NR:(nb + j + 1) * NR], G[:, j:NR * W:W], ACT.Square,
-                         bias=t("nU")[:, j:j + 1], accum_out=t("E")[:, j:j + 1]).then_inc(s("se"), 1)
+            V.tensor_reduce(t("NS")[:, j:j + 1], G[:, j:NR * W:W], AxisListType.X, ALU.add,
+                            negate=True).then_inc(s("sns"), 1)
         for j in range(nb):
             V.tensor_reduce(t("SQ")[:, j:j + 1], G[:, nb + j:NR * W:W], AxisListType.X, ALU.add).then_inc(s("ssq"), 1)
         V.wait_ge(s("ssq"), nb)
-        V.tensor_scalar(t("w")[:], t("SQ")[:], EPS, 1.0 / 128.0, ALU.add, ALU.mult).then_inc(s("sw"), 1)
-        V.wait_ge(s("snu"), nb)
-        V.tensor_scalar(t("mu")[:], t("nU")[:], 32.0, None, ALU.mult).then_inc(s("smu"), 1)
+        V.tensor_scalar(t("w")[:], t("SQ")[:], 0.5, EPS / 128.0, ALU.mult, ALU.add).then_inc(s("sw"), 1)
+        V.wait_ge(s("sns"), nb)
+        V.tensor_scalar(t("mu")[:], t("NS")[:], 32.0, None, ALU.mult).then_inc(s("smu"), 1)
+
+    def vsum(p):
+        lo, hi, nb, W, G, t, s = names(p)
         V.wait_ge(s("se"), nb)
         V.wait_ge(s("sw"), 1)
         V.tensor_tensor(t("v")[:], t("E")[:], t("w")[:], ALU.add).then_inc(s("sv"), 1)
-        A.wait_ge(s("sv"), 1)
-        A.activation(t("sd")[:], t("v")[:], ACT.Sqrt, scale=128.0).then_inc(s("ssd"), 1)
+
+    def fin(p):
+        lo, hi, nb, W, G, t, s = names(p)
         V.wait_ge(s("ssd"), 1)
         V.reciprocal(t("r")[:], t("sd")[:]).then_inc(s("sr"), 1)
         V.wait_ge(s("sr"), 1)
@@ -185,6 +192,24 @@ def rank_program(g, core, T, topo):
                             ALU.subtract, ALU.mult).then_inc(S["ap%d" % b], 1)
             g.tensor.wait_ge(S["ap%d" % b], 1)
             g.tensor.matmul(T["yo%d" % b][:, 0:P], T.yT[:, blk(b)], ident, True, True).then_inc(S["bt%d" % b], 1)
+
+    prep(0)
+    vsum(0)
+    for p in range(NP):
+        if p + 1 < NP:
+            prep(p + 1)
+        fin(p)
+        if p + 1 < NP:
+            vsum(p + 1)
+    for p in range(NP):
+        lo, hi, nb, W, G, t, s = names(p)
+        arrived(A, p)
+        A.wait_ge(s("sns"), nb)
+        for j in range(nb):
+            A.activation(T["js%d" % p][:, j * NR:(j + 1) * NR], G[:, j:NR * W:W], ACT.Square,
+                         bias=t("NS")[:, j:j + 1], scale=8.0, accum_out=t("E")[:, j:j + 1]).then_inc(s("se"), 1)
+        A.wait_ge(s("sv"), 1)
+        A.activation(t("sd")[:], t("v")[:], ACT.Sqrt, scale=128.0).then_inc(s("ssd"), 1)
 
     for b in range(4):
         A.wait_ge(S["bt%d" % b], 1)

@@ -28,10 +28,12 @@ for _b in range(4):
 for _p, (_lo, _hi) in enumerate(PARTS):
     _nb = _hi - _lo
     SCRATCH["G%d" % _p] = ("sbuf", [P, NR * _width(_nb)], "float32")
-    SCRATCH["js%d" % _p] = ("sbuf", [P, _nb * NR], "float32")
+    for _n in ("D", "D2"):
+        SCRATCH["%s%d" % (_n, _p)] = ("sbuf", [P, _nb * NR], "float32")
     for _n in ("NS", "E", "SQ", "w", "v", "sd", "r", "mu"):
         SCRATCH["%s%d" % (_n, _p)] = ("sbuf", [P, _nb], "float32")
-    SEMAPHORES += [n + str(_p) for n in ("pad", "on", "off", "sns", "se", "ssq", "sw", "smu", "sv", "ssd", "sr")]
+    SEMAPHORES += [n + str(_p) for n in ("pad", "on", "off", "sns", "sdv", "sd2", "se", "ssq", "sw", "smu", "sv",
+                                         "ssd", "sr")]
 
 
 def _bits(mask):
@@ -83,7 +85,7 @@ def rank_program(g, core, T, topo):
     S = T.sem
     ACT = ActivationFunctionType
     ALU = AluOpType
-    V, A = g.vector, g.scalar
+    V, A, PE = g.vector, g.scalar, g.tensor
     cores = list(T.cores)
     slot, on, off = _plan(cores, topo)
     me = slot[core]
@@ -103,6 +105,11 @@ def rank_program(g, core, T, topo):
              for ds, e in transfers], local_sem=S.sent)
         return sum(len(e) for ds, e in transfers)
 
+    def names(p):
+        lo, hi = PARTS[p]
+        return (lo, hi, hi - lo, _width(hi - lo), T["G%d" % p],
+                lambda n: T["%s%d" % (n, p)], lambda n: S["%s%d" % (n, p)])
+
     for b in range(4):
         q = g.sync if b % 2 == 0 else g.scalar
         q.dma_start(T.xs[:, blk(b)], T.x[:, blk(b)]).then_inc(S["ld%d" % b], 16)
@@ -110,20 +117,20 @@ def rank_program(g, core, T, topo):
     V.memset(T.idx[:, P:P + 1], -1.0 / 32768.0).then_inc(S.c2, 1)
     g.wait_ge(S.c1, 1)
     g.affine_select(ident, T.ones[:], [[-1, P]], ALU.is_equal, 0.0, 0, 1).then_inc(S.c2, 1)
-    for p, (lo, hi) in enumerate(PARTS):
-        nb, W = hi - lo, _width(hi - lo)
+    for p in range(NP):
+        lo, hi, nb, W, G, t, s = names(p)
         if W > 2 * nb:
-            V.memset(T["G%d" % p][:, me * W + 2 * nb:(me + 1) * W], 0.0).then_inc(S["pad%d" % p], 1)
+            V.memset(G[:, me * W + 2 * nb:(me + 1) * W], 0.0).then_inc(s("pad"), 1)
 
-    g.tensor.wait_ge(S.c2, 2)
-    for p, (lo, hi) in enumerate(PARTS):
-        nb, W, G = hi - lo, _width(hi - lo), T["G%d" % p]
+    PE.wait_ge(S.c2, 2)
+    for p in range(NP):
+        lo, hi, nb, W, G, t, s = names(p)
         for b in range(lo, hi):
             j = b - lo
             xT = T["xT%d" % b]
             ucol = G[:, me * W + j:me * W + j + 1]
-            g.tensor.wait_ge(S["ld%d" % b], 16)
-            g.tensor.matmul(xT[:, 0:P + 1], T.xs[:, blk(b)], T.idx[:, 0:P + 1], True, True).then_inc(S["tr%d" % b], 1)
+            PE.wait_ge(S["ld%d" % b], 16)
+            PE.matmul(xT[:, 0:P + 1], T.xs[:, blk(b)], T.idx[:, 0:P + 1], True, True).then_inc(S["tr%d" % b], 1)
             V.wait_ge(S["tr%d" % b], 1)
             V.tensor_copy(ucol, xT[:, P:P + 1]).then_inc(S["ucp%d" % b], 1)
             A.wait_ge(S["tr%d" % b], 1)
@@ -132,26 +139,21 @@ def rank_program(g, core, T, topo):
                          accum_out=G[:, me * W + nb + j:me * W + nb + j + 1]).then_inc(S["sq%d" % b], 1)
 
     sent = 0
-    for p, (lo, hi) in enumerate(PARTS):
-        nb, W, G = hi - lo, _width(hi - lo), T["G%d" % p]
+    for p in range(NP):
+        lo, hi, nb, W, G, t, s = names(p)
         if W > 2 * nb:
-            g.wait_ge(S["pad%d" % p], 1)
+            g.wait_ge(s("pad"), 1)
         for b in range(lo, hi):
             g.wait_ge(S["ucp%d" % b], 1)
             g.wait_ge(S["sq%d" % b], 1)
         for call in on[core]:
-            sent += send(call, G[:, me * W:(me + 1) * W], S["on%d" % p])
+            sent += send(call, G[:, me * W:(me + 1) * W], s("on"))
     if core in off:
-        for p, (lo, hi) in enumerate(PARTS):
-            W, G = _width(hi - lo), T["G%d" % p]
-            g.wait_ge(S["on%d" % p], n_on)
-            sent += send(off[core], G[:, here[0] * W:(here[-1] + 1) * W], S["off%d" % p])
+        for p in range(NP):
+            lo, hi, nb, W, G, t, s = names(p)
+            g.wait_ge(s("on"), n_on)
+            sent += send(off[core], G[:, here[0] * W:(here[-1] + 1) * W], s("off"))
     g.wait_ge(S.sent, sent)
-
-    def names(p):
-        lo, hi = PARTS[p]
-        return (lo, hi, hi - lo, _width(hi - lo), T["G%d" % p],
-                lambda n: T["%s%d" % (n, p)], lambda n: S["%s%d" % (n, p)])
 
     def arrived(q, p):
         lo, hi, nb, W, G, t, s = names(p)
@@ -161,7 +163,7 @@ def rank_program(g, core, T, topo):
             q.wait_ge(S["ucp%d" % b], 1)
             q.wait_ge(S["sq%d" % b], 1)
 
-    def prep(p):
+    def sums(p):
         lo, hi, nb, W, G, t, s = names(p)
         arrived(V, p)
         for j in range(nb):
@@ -169,20 +171,15 @@ def rank_program(g, core, T, topo):
                             negate=True).then_inc(s("sns"), 1)
         for j in range(nb):
             V.tensor_reduce(t("SQ")[:, j:j + 1], G[:, nb + j:NR * W:W], AxisListType.X, ALU.add).then_inc(s("ssq"), 1)
-        V.wait_ge(s("ssq"), nb)
-        V.tensor_scalar(t("w")[:], t("SQ")[:], 0.5, EPS / 128.0, ALU.mult, ALU.add).then_inc(s("sw"), 1)
+
+    def mean(p):
+        lo, hi, nb, W, G, t, s = names(p)
         V.wait_ge(s("sns"), nb)
         V.tensor_scalar(t("mu")[:], t("NS")[:], 32.0, None, ALU.mult).then_inc(s("smu"), 1)
 
-    def vsum(p):
-        lo, hi, nb, W, G, t, s = names(p)
-        V.wait_ge(s("se"), nb)
-        V.wait_ge(s("sw"), 1)
-        V.tensor_tensor(t("v")[:], t("E")[:], t("w")[:], ALU.add).then_inc(s("sv"), 1)
-
     def fin(p):
         lo, hi, nb, W, G, t, s = names(p)
-        V.wait_ge(s("ssd"), 1)
+        V.wait_ge(s("ssd"), nb if p == 0 else 1)
         V.reciprocal(t("r")[:], t("sd")[:]).then_inc(s("sr"), 1)
         V.wait_ge(s("sr"), 1)
         V.wait_ge(s("smu"), 1)
@@ -190,26 +187,48 @@ def rank_program(g, core, T, topo):
             j = b - lo
             V.tensor_scalar(T.yT[:, blk(b)], T["xT%d" % b][:, 0:P], t("mu")[:, j:j + 1], t("r")[:, j:j + 1],
                             ALU.subtract, ALU.mult).then_inc(S["ap%d" % b], 1)
-            g.tensor.wait_ge(S["ap%d" % b], 1)
-            g.tensor.matmul(T["yo%d" % b][:, 0:P], T.yT[:, blk(b)], ident, True, True).then_inc(S["bt%d" % b], 1)
+            PE.wait_ge(S["ap%d" % b], 1)
+            PE.matmul(T["yo%d" % b][:, 0:P], T.yT[:, blk(b)], ident, True, True).then_inc(S["bt%d" % b], 1)
 
-    prep(0)
-    vsum(0)
-    for p in range(NP):
-        if p + 1 < NP:
-            prep(p + 1)
-        fin(p)
-        if p + 1 < NP:
-            vsum(p + 1)
-    for p in range(NP):
+    lo, hi, nb, W, G, t, s = names(0)
+    sums(0)
+    V.wait_ge(s("ssq"), nb)
+    V.tensor_scalar(t("w")[:], t("SQ")[:], 64.0, EPS, ALU.mult, ALU.add).then_inc(s("sw"), 1)
+    mean(0)
+    arrived(A, 0)
+    A.wait_ge(s("sns"), nb)
+    for j in range(nb):
+        A.activation(t("D")[:, j * NR:(j + 1) * NR], G[:, j:NR * W:W], ACT.Square,
+                     bias=t("NS")[:, j:j + 1], scale=8.0, accum_out=t("E")[:, j:j + 1]).then_inc(s("se"), 1)
+    A.wait_ge(s("se"), nb)
+    A.wait_ge(s("sw"), 1)
+    for j in range(nb):
+        A.activation(t("sd")[:, j:j + 1], t("E")[:, j:j + 1], ACT.Sqrt, bias=t("w")[:, j:j + 1],
+                     scale=128.0).then_inc(s("ssd"), 1)
+
+    for p in range(1, NP):
         lo, hi, nb, W, G, t, s = names(p)
-        arrived(A, p)
-        A.wait_ge(s("sns"), nb)
+        sums(p)
+        V.wait_ge(s("sns"), nb)
         for j in range(nb):
-            A.activation(T["js%d" % p][:, j * NR:(j + 1) * NR], G[:, j:NR * W:W], ACT.Square,
-                         bias=t("NS")[:, j:j + 1], scale=8.0, accum_out=t("E")[:, j:j + 1]).then_inc(s("se"), 1)
+            V.tensor_scalar(t("D")[:, j * NR:(j + 1) * NR], G[:, j:NR * W:W], 8.0, t("NS")[:, j:j + 1],
+                            ALU.mult, ALU.add).then_inc(s("sdv"), 1)
+        V.wait_ge(s("ssq"), nb)
+        V.tensor_scalar(t("w")[:], t("SQ")[:], 0.5, EPS / 128.0, ALU.mult, ALU.add).then_inc(s("sw"), 1)
+        mean(p)
+        V.wait_ge(s("sdv"), nb)
+        V.tensor_tensor(t("D2")[:], t("D")[:], t("D")[:], ALU.mult).then_inc(s("sd2"), 1)
+        V.wait_ge(s("sd2"), 1)
+        for j in range(nb):
+            V.tensor_reduce(t("E")[:, j:j + 1], t("D2")[:, j * NR:(j + 1) * NR], AxisListType.X,
+                            ALU.add).then_inc(s("se"), 1)
+        V.wait_ge(s("se"), nb)
+        V.wait_ge(s("sw"), 1)
+        V.tensor_tensor(t("v")[:], t("E")[:], t("w")[:], ALU.add).then_inc(s("sv"), 1)
         A.wait_ge(s("sv"), 1)
         A.activation(t("sd")[:], t("v")[:], ACT.Sqrt, scale=128.0).then_inc(s("ssd"), 1)
+    for p in range(NP):
+        fin(p)
 
     for b in range(4):
         A.wait_ge(S["bt%d" % b], 1)

@@ -16,24 +16,27 @@ SCRATCH = {
     "xs": ("sbuf", [P, 512], "float32"),
     "ones": ("sbuf", [P, P], "float32"),
     "idx": ("sbuf", [P, 132], "float32"),
+    "idn": ("sbuf", [P, P], "float32"),
     "junk": ("sbuf", [P, 512], "float32"),
-    "yT": ("sbuf", [P, 512], "float32"),
+    "zr": ("sbuf", [P, 512], "float32"),
+    "dg": ("sbuf", [P, 512], "float32"),
     "ys": ("sbuf", [P, 512], "float32"),
+    "dm0": ("sbuf", [P, 1], "float32"),
 }
-SEMAPHORES = ["c1", "c2", "sent"]
+SEMAPHORES = ["c1", "c2", "c3", "sent", "sdm0"]
 for _b in range(4):
     SCRATCH["xT%d" % _b] = ("psum", [P, 512], "float32")
     SCRATCH["yo%d" % _b] = ("psum", [P, 512], "float32")
-    SEMAPHORES += [n + str(_b) for n in ("ld", "tr", "ucp", "sq", "ap", "bt", "cp", "st")]
+    SEMAPHORES += [n + str(_b) for n in ("ld", "tr", "ucp", "sq", "ap", "dgs", "bt", "cp", "st",
+                                         "jns", "jd", "jd2", "jv")]
 for _p, (_lo, _hi) in enumerate(PARTS):
     _nb = _hi - _lo
     SCRATCH["G%d" % _p] = ("sbuf", [P, NR * _width(_nb)], "float32")
-    for _n in ("D", "D2"):
-        SCRATCH["%s%d" % (_n, _p)] = ("sbuf", [P, _nb * NR], "float32")
-    for _n in ("NS", "E", "SQ", "w", "v", "sd", "r", "mu"):
+    SCRATCH["D%d" % _p] = ("sbuf", [P, _nb * NR], "float32")
+    SCRATCH["X%d" % _p] = ("sbuf", [P, _nb * 2 * NR], "float32")
+    for _n in ("NS", "E", "SQ", "w", "v", "sd", "r"):
         SCRATCH["%s%d" % (_n, _p)] = ("sbuf", [P, _nb], "float32")
-    SEMAPHORES += [n + str(_p) for n in ("pad", "on", "off", "sns", "sdv", "sd2", "se", "ssq", "sw", "smu", "sv",
-                                         "ssd", "sr")]
+    SEMAPHORES += [n + str(_p) for n in ("pad", "on", "off", "sns", "se", "ssq", "sw", "sv", "ssd", "sr", "sqp")]
 
 
 def _bits(mask):
@@ -85,6 +88,7 @@ def rank_program(g, core, T, topo):
     S = T.sem
     ACT = ActivationFunctionType
     ALU = AluOpType
+    AX = AxisListType.X
     V, A, PE = g.vector, g.scalar, g.tensor
     cores = list(T.cores)
     slot, on, off = _plan(cores, topo)
@@ -92,7 +96,6 @@ def rank_program(g, core, T, topo):
     here = sorted(slot[d] for d in cores if topo.chip(d) == topo.chip(core))
     n_on = sum(len(e) for c in cores if c != core for call in on[c] for ds, e in call if core in ds)
     n_off = sum(len(e) for c in off for ds, e in off[c] if core in ds)
-    ident = T.idx[:, 0:P]
     NP = len(PARTS)
 
     def blk(b):
@@ -113,14 +116,15 @@ def rank_program(g, core, T, topo):
     for b in range(4):
         q = g.sync if b % 2 == 0 else g.scalar
         q.dma_start(T.xs[:, blk(b)], T.x[:, blk(b)]).then_inc(S["ld%d" % b], 16)
-    V.memset(T.ones[:], 1.0).then_inc(S.c1, 1)
-    V.memset(T.idx[:, P:P + 1], -1.0 / 32768.0).then_inc(S.c2, 1)
+    V.memset(T.ones[:], 1.0 - 1.0 / 128.0).then_inc(S.c1, 1)
+    V.memset(T.idx[:, P:P + 1], -1.0 / 1024.0).then_inc(S.c2, 1)
     g.wait_ge(S.c1, 1)
-    g.affine_select(ident, T.ones[:], [[-1, P]], ALU.is_equal, 0.0, 0, 1).then_inc(S.c2, 1)
+    g.affine_select(T.idx[:, 0:P], T.ones[:], [[-1, P]], ALU.is_equal, -1.0 / 128.0, 0, 1).then_inc(S.c2, 1)
     for p in range(NP):
         lo, hi, nb, W, G, t, s = names(p)
-        if W > 2 * nb:
-            V.memset(G[:, me * W + 2 * nb:(me + 1) * W], 0.0).then_inc(s("pad"), 1)
+        V.memset(G[:, me * W + 2 * nb:(me + 1) * W], 0.0).then_inc(s("pad"), 1)
+    V.wait_ge(S.c2, 2)
+    V.tensor_scalar(T.idn[:], T.idx[:, 0:P], 1.0 / 128.0, None, ALU.add).then_inc(S.c3, 1)
 
     PE.wait_ge(S.c2, 2)
     for p in range(NP):
@@ -128,24 +132,20 @@ def rank_program(g, core, T, topo):
         for b in range(lo, hi):
             j = b - lo
             xT = T["xT%d" % b]
-            ucol = G[:, me * W + j:me * W + j + 1]
             PE.wait_ge(S["ld%d" % b], 16)
             PE.matmul(xT[:, 0:P + 1], T.xs[:, blk(b)], T.idx[:, 0:P + 1], True, True).then_inc(S["tr%d" % b], 1)
-            V.wait_ge(S["tr%d" % b], 1)
-            V.tensor_copy(ucol, xT[:, P:P + 1]).then_inc(S["ucp%d" % b], 1)
             A.wait_ge(S["tr%d" % b], 1)
-            A.wait_ge(S["ucp%d" % b], 1)
-            A.activation(T.junk[:, blk(b)], xT[:, 0:P], ACT.Square, bias=ucol, scale=1.0 / 256.0,
+            A.activation(T.junk[:, blk(b)], xT[:, 0:P], ACT.Square, scale=1.0 / 8.0,
                          accum_out=G[:, me * W + nb + j:me * W + nb + j + 1]).then_inc(S["sq%d" % b], 1)
+            A.activation(G[:, me * W + j:me * W + j + 1], xT[:, P:P + 1], ACT.Copy).then_inc(S["ucp%d" % b], 1)
 
     sent = 0
     for p in range(NP):
         lo, hi, nb, W, G, t, s = names(p)
-        if W > 2 * nb:
-            g.wait_ge(s("pad"), 1)
+        g.wait_ge(s("pad"), 1)
         for b in range(lo, hi):
-            g.wait_ge(S["ucp%d" % b], 1)
             g.wait_ge(S["sq%d" % b], 1)
+            g.wait_ge(S["ucp%d" % b], 1)
         for call in on[core]:
             sent += send(call, G[:, me * W:(me + 1) * W], s("on"))
     if core in off:
@@ -163,76 +163,83 @@ def rank_program(g, core, T, topo):
             q.wait_ge(S["ucp%d" % b], 1)
             q.wait_ge(S["sq%d" % b], 1)
 
-    def sums(p):
+    def diags(p):
         lo, hi, nb, W, G, t, s = names(p)
-        arrived(V, p)
-        for j in range(nb):
-            V.tensor_reduce(t("NS")[:, j:j + 1], G[:, j:NR * W:W], AxisListType.X, ALU.add,
-                            negate=True).then_inc(s("sns"), 1)
-        for j in range(nb):
-            V.tensor_reduce(t("SQ")[:, j:j + 1], G[:, nb + j:NR * W:W], AxisListType.X, ALU.add).then_inc(s("ssq"), 1)
-
-    def mean(p):
-        lo, hi, nb, W, G, t, s = names(p)
-        V.wait_ge(s("sns"), nb)
-        V.tensor_scalar(t("mu")[:], t("NS")[:], 32.0, None, ALU.mult).then_inc(s("smu"), 1)
-
-    def fin(p):
-        lo, hi, nb, W, G, t, s = names(p)
-        V.wait_ge(s("ssd"), nb if p == 0 else 1)
-        V.reciprocal(t("r")[:], t("sd")[:]).then_inc(s("sr"), 1)
-        V.wait_ge(s("sr"), 1)
-        V.wait_ge(s("smu"), 1)
+        A.wait_ge(s("ssd"), 1)
         for b in range(lo, hi):
             j = b - lo
-            V.tensor_scalar(T.yT[:, blk(b)], T["xT%d" % b][:, 0:P], t("mu")[:, j:j + 1], t("r")[:, j:j + 1],
-                            ALU.subtract, ALU.mult).then_inc(S["ap%d" % b], 1)
-            PE.wait_ge(S["ap%d" % b], 1)
-            PE.matmul(T["yo%d" % b][:, 0:P], T.yT[:, blk(b)], ident, True, True).then_inc(S["bt%d" % b], 1)
+            A.activation(T.dg[:, blk(b)], T.idn[:], ACT.Copy, scale=t("sd")[:, j:j + 1]).then_inc(S["dgs%d" % b], 1)
 
-    lo, hi, nb, W, G, t, s = names(0)
-    sums(0)
-    V.wait_ge(s("ssq"), nb)
-    V.tensor_scalar(t("w")[:], t("SQ")[:], 64.0, EPS, ALU.mult, ALU.add).then_inc(s("sw"), 1)
-    mean(0)
+    lo, hi, nb, W0, G0, t0, s0 = names(0)
+    arrived(V, 0)
+    V.tensor_reduce(t0("NS")[:], G0[:, 0:NR * W0:W0], AX, ALU.add, negate=True).then_inc(s0("sns"), 1)
+    V.tensor_reduce(t0("SQ")[:], G0[:, 1:NR * W0:W0], AX, ALU.add).then_inc(s0("ssq"), 1)
+    V.wait_ge(s0("ssq"), 1)
+    V.tensor_scalar(t0("w")[:], t0("SQ")[:], 1.0 / 16.0, EPS, ALU.mult, ALU.add).then_inc(s0("sw"), 1)
+    V.wait_ge(s0("sns"), 1)
+    V.tensor_scalar(T.dm0[:], G0[:, me * W0:me * W0 + 1], 8.0, t0("NS")[:, 0:1], ALU.mult, ALU.add).then_inc(S.sdm0, 1)
     arrived(A, 0)
-    A.wait_ge(s("sns"), nb)
-    for j in range(nb):
-        A.activation(t("D")[:, j * NR:(j + 1) * NR], G[:, j:NR * W:W], ACT.Square,
-                     bias=t("NS")[:, j:j + 1], scale=8.0, accum_out=t("E")[:, j:j + 1]).then_inc(s("se"), 1)
-    A.wait_ge(s("se"), nb)
-    A.wait_ge(s("sw"), 1)
-    for j in range(nb):
-        A.activation(t("sd")[:, j:j + 1], t("E")[:, j:j + 1], ACT.Sqrt, bias=t("w")[:, j:j + 1],
-                     scale=128.0).then_inc(s("ssd"), 1)
+    A.wait_ge(s0("sns"), 1)
+    A.activation(t0("D")[:], G0[:, 0:NR * W0:W0], ACT.Square, bias=t0("NS")[:, 0:1], scale=8.0,
+                 accum_out=t0("E")[:, 0:1]).then_inc(s0("se"), 1)
+    A.wait_ge(s0("se"), 1)
+    A.wait_ge(s0("sw"), 1)
+    A.activation(t0("sd")[:], t0("E")[:], ACT.Sqrt, bias=t0("w")[:, 0:1], scale=0.125).then_inc(s0("ssd"), 1)
+    A.wait_ge(S.c3, 1)
+    diags(0)
 
-    for p in range(1, NP):
-        lo, hi, nb, W, G, t, s = names(p)
-        sums(p)
-        V.wait_ge(s("sns"), nb)
-        for j in range(nb):
-            V.tensor_scalar(t("D")[:, j * NR:(j + 1) * NR], G[:, j:NR * W:W], 8.0, t("NS")[:, j:j + 1],
-                            ALU.mult, ALU.add).then_inc(s("sdv"), 1)
-        V.wait_ge(s("ssq"), nb)
-        V.tensor_scalar(t("w")[:], t("SQ")[:], 0.5, EPS / 128.0, ALU.mult, ALU.add).then_inc(s("sw"), 1)
-        mean(p)
-        V.wait_ge(s("sdv"), nb)
-        V.tensor_tensor(t("D2")[:], t("D")[:], t("D")[:], ALU.mult).then_inc(s("sd2"), 1)
-        V.wait_ge(s("sd2"), 1)
-        for j in range(nb):
-            V.tensor_reduce(t("E")[:, j:j + 1], t("D2")[:, j * NR:(j + 1) * NR], AxisListType.X,
-                            ALU.add).then_inc(s("se"), 1)
-        V.wait_ge(s("se"), nb)
-        V.wait_ge(s("sw"), 1)
-        V.tensor_tensor(t("v")[:], t("E")[:], t("w")[:], ALU.add).then_inc(s("sv"), 1)
-        A.wait_ge(s("sv"), 1)
-        A.activation(t("sd")[:], t("v")[:], ACT.Sqrt, scale=128.0).then_inc(s("ssd"), 1)
-    for p in range(NP):
-        fin(p)
+    lo, hi, nb, W, G, t, s = names(1)
+    X, D = t("X"), t("D")
+    arrived(V, 1)
+    for j in range(nb):
+        V.tensor_reduce(t("NS")[:, j:j + 1], G[:, j:NR * W:W], AX, ALU.add, negate=True).then_inc(S["jns%d" % j], 1)
+    for j in range(nb):
+        V.tensor_scalar(X[:, j * 16 + 8:j * 16 + 16], G[:, nb + j:NR * W:W], 0.5, EPS,
+                        ALU.mult, ALU.add).then_inc(s("sqp"), 1)
+    for j in range(nb):
+        V.wait_ge(S["jns%d" % j], 1)
+        V.tensor_scalar(D[:, j * NR:(j + 1) * NR], G[:, j:NR * W:W], 8.0, t("NS")[:, j:j + 1],
+                        ALU.mult, ALU.add).then_inc(S["jd%d" % j], 1)
+    V.wait_ge(s0("se"), 1)
+    V.wait_ge(s0("sw"), 1)
+    V.tensor_scalar(t0("v")[:], t0("E")[:], 0.125, t0("w")[:, 0:1], ALU.mult, ALU.add).then_inc(s0("sv"), 1)
+    for j in range(nb):
+        V.wait_ge(S["jd%d" % j], 1)
+        V.tensor_tensor(X[:, j * 16:j * 16 + 8], D[:, j * NR:(j + 1) * NR], D[:, j * NR:(j + 1) * NR],
+                        ALU.mult).then_inc(S["jd2%d" % j], 1)
+    V.wait_ge(s0("sv"), 1)
+    V.reciprocal(t0("r")[:], t0("v")[:]).then_inc(s0("sr"), 1)
+    V.wait_ge(s("sqp"), nb)
+    for j in range(nb):
+        V.wait_ge(S["jd2%d" % j], 1)
+        V.tensor_reduce(t("v")[:, j:j + 1], X[:, j * 16:(j + 1) * 16], AX, ALU.add).then_inc(S["jv%d" % j], 1)
+    V.wait_ge(s0("sr"), 1)
+    V.wait_ge(S.sdm0, 1)
+    V.tensor_scalar(T.zr[:, blk(0)], T.xT0[:, 0:P], T.dm0[:, 0:1], t0("r")[:, 0:1],
+                    ALU.subtract, ALU.mult).then_inc(S.ap0, 1)
+    for j in range(nb):
+        V.wait_ge(S["jv%d" % j], 1)
+        A.wait_ge(S["jv%d" % j], 1)
+    V.reciprocal(t("r")[:], t("v")[:]).then_inc(s("sr"), 1)
+    A.activation(t("sd")[:], t("v")[:], ACT.Sqrt, scale=8.0).then_inc(s("ssd"), 1)
+    diags(1)
+    V.wait_ge(s("sr"), 1)
+    for b in range(lo, hi):
+        j = b - lo
+        V.tensor_scalar(T.zr[:, blk(b)], T["xT%d" % b][:, 0:P], D[:, j * NR + me:j * NR + me + 1], t("r")[:, j:j + 1],
+                        ALU.subtract, ALU.mult).then_inc(S["ap%d" % b], 1)
 
     for b in range(4):
-        A.wait_ge(S["bt%d" % b], 1)
-        A.activation(T.ys[:, blk(b)], T["yo%d" % b][:, 0:P], ACT.Copy).then_inc(S["cp%d" % b], 1)
+        PE.wait_ge(S["ap%d" % b], 1)
+        PE.wait_ge(S["dgs%d" % b], 1)
+        PE.matmul(T["yo%d" % b][:, 0:P], T.zr[:, blk(b)], T.dg[:, blk(b)], True, True).then_inc(S["bt%d" % b], 1)
+    for b in range(4):
+        if b % 2 == 0:
+            A.wait_ge(S["bt%d" % b], 1)
+            A.activation(T.ys[:, blk(b)], T["yo%d" % b][:, 0:P], ACT.Copy).then_inc(S["cp%d" % b], 1)
+        else:
+            V.wait_ge(S["bt%d" % b], 1)
+            V.tensor_copy(T.ys[:, blk(b)], T["yo%d" % b][:, 0:P]).then_inc(S["cp%d" % b], 1)
         g.sync.wait_ge(S["cp%d" % b], 1)
         g.sync.dma_start(T.y[:, blk(b)], T.ys[:, blk(b)]).then_inc(S["st%d" % b], 16)
     for b in range(4):

@@ -4,6 +4,7 @@ from concourse.mybir import dt, AluOpType, AxisListType, ActivationFunctionType
 
 P = 128
 NR = 8
+SIM = 64
 EPS = 0.01
 PARTS = ((0, 1), (1, 4))
 
@@ -19,24 +20,24 @@ SCRATCH = {
     "idn": ("sbuf", [P, P], "float32"),
     "junk": ("sbuf", [P, 512], "float32"),
     "zr": ("sbuf", [P, 512], "float32"),
+    "dgs8": ("sbuf", [P, 512], "float32"),
     "dg": ("sbuf", [P, 512], "float32"),
     "ys": ("sbuf", [P, 512], "float32"),
-    "dm0": ("sbuf", [P, 1], "float32"),
+    "Dj": ("sbuf", [P, 4 * NR], "float32"),
 }
-SEMAPHORES = ["c1", "c2", "c3", "sent", "sdm0"]
+for _n in ("NS", "SQ", "wr", "w8", "E", "v8", "r8", "tt", "dm", "S8", "s2", "rr", "k8", "k16", "ke"):
+    SCRATCH[_n] = ("sbuf", [P, 4], "float32")
+SEMAPHORES = ["c1", "c2", "c3", "sent", "hs", "h1", "h2", "hk", "hd"]
 for _b in range(4):
     SCRATCH["xT%d" % _b] = ("psum", [P, 512], "float32")
     SCRATCH["yo%d" % _b] = ("psum", [P, 512], "float32")
     SEMAPHORES += [n + str(_b) for n in ("ld", "tr", "ucp", "sq", "ap", "dgs", "bt", "cp", "st",
-                                         "jns", "jd", "jd2", "jv")]
+                                         "jns", "jsq", "jwr", "jdm", "je", "jt")]
 for _p, (_lo, _hi) in enumerate(PARTS):
     _nb = _hi - _lo
     SCRATCH["G%d" % _p] = ("sbuf", [P, NR * _width(_nb)], "float32")
-    SCRATCH["D%d" % _p] = ("sbuf", [P, _nb * NR], "float32")
-    SCRATCH["X%d" % _p] = ("sbuf", [P, _nb * 2 * NR], "float32")
-    for _n in ("NS", "E", "SQ", "w", "v", "sd", "r"):
-        SCRATCH["%s%d" % (_n, _p)] = ("sbuf", [P, _nb], "float32")
-    SEMAPHORES += [n + str(_p) for n in ("pad", "on", "off", "sns", "se", "ssq", "sw", "sv", "ssd", "sr", "sqp")]
+    SCRATCH["own%d" % _p] = ("sbuf", [P, _width(_nb)], "float32")
+    SEMAPHORES += [n + str(_p) for n in ("pad", "on", "off", "sw", "sv", "sr")]
 
 
 def _bits(mask):
@@ -54,64 +55,125 @@ def _pow2(n):
     return k
 
 
+def _deal(dests, engines):
+    if not dests:
+        return []
+    k = _pow2(len(engines) // len(dests))
+    return [([d], engines[i * k:(i + 1) * k]) for i, d in enumerate(dests)]
+
+
+def _pick(pool, load, d, topo):
+    same = [f for f in pool if topo.die(f) == topo.die(d)] or pool
+    return min(same, key=lambda f: (len(load[f]), pool.index(f)))
+
+
 def _plan(cores, topo):
     order = sorted(cores, key=lambda c: (topo.chip(c), cores.index(c)))
     slot = {c: i for i, c in enumerate(order)}
-    on, off = {}, {}
-    for c in cores:
-        here = [d for d in cores if topo.chip(d) == topo.chip(c)]
-        there = [d for d in cores if topo.chip(d) != topo.chip(c)]
-        relays = [d for d in here if all(topo.may_write(d, e) for e in there)]
-        peers = [d for d in here if d != c]
-        far = _bits(topo.mask(c, there[0]))
-        near = [e for e in _bits(topo.mask(c, peers[0])) if e not in far]
-        urgent = [d for d in peers if d in relays]
-        rest = [d for d in peers if d not in relays]
-        k = _pow2(len(far) // max(1, len(urgent)))
-        on[c] = [[([d], far[i * k:(i + 1) * k]) for i, d in enumerate(urgent)]]
-        if rest:
-            on[c].append([(rest, near[:_pow2(len(near))])])
-        if c in relays:
-            mine = []
-            for i, d in enumerate(there):
-                same = [r for r in relays if topo.die(r) == topo.die(d)]
-                if (same[0] if same else relays[i % len(relays)]) == c:
-                    mine.append(d)
-            k = _pow2(len(far) // max(1, len(mine)))
-            off[c] = [([d], far[i * k:(i + 1) * k]) for i, d in enumerate(mine)]
-    return slot, on, off
+    hop = [{} for p in PARTS]
+    fwd = [{} for p in PARTS]
+    back = [False for p in PARTS]
+    ident = {}
+    for ch in sorted(set(topo.chip(c) for c in cores)):
+        here = [c for c in cores if topo.chip(c) == ch]
+        there = [c for c in cores if topo.chip(c) != ch]
+        able = [c for c in range(SIM) if topo.chip(c) == ch and all(topo.may_write(c, d) for d in there)]
+        relays = [c for c in able if c in here]
+        helpers = [c for c in able if c not in here]
+
+        def engines(c):
+            peer = [d for d in here if d != c][0]
+            out = _bits(topo.mask(c, there[0]))
+            return out, [e for e in _bits(topo.mask(c, peer)) if e not in out]
+
+        for p in range(len(PARTS)):
+            back[p] = p == 0 and len(helpers) > 0
+            fw = helpers if back[p] else relays
+            far = {f: [] for f in fw}
+            near = {f: [] for f in fw}
+            for d in there:
+                far[_pick(fw, far, d, topo)].append(d)
+            for d in here:
+                if back[p]:
+                    near[_pick(fw, near, d, topo)].append(d)
+            for c in here:
+                out, others = engines(c)
+                hop[p][c] = [_deal([f for f in fw if f != c], out)]
+                rest = [d for d in here if d != c and d not in fw]
+                if rest and not back[p]:
+                    hop[p][c].append([(rest, others[:_pow2(len(others))])])
+            for f in fw:
+                out, others = engines(f)
+                fwd[p][f] = _deal(far[f], out) + _deal(near[f], others)
+        give = {f: [] for f in helpers}
+        for d in here:
+            if helpers:
+                give[_pick(helpers, give, d, topo)].append(d)
+        for f in helpers:
+            out, others = engines(f)
+            ident[f] = _deal(give[f], out + others)
+    return slot, hop, fwd, back, ident
 
 
 def rank_program(g, core, T, topo):
-    if T.rank_of(core) is None:
+    cores = list(T.cores)
+    slot, hop, fwd, back, ident = _plan(cores, topo)
+    is_rank = T.rank_of(core) is not None
+    if not is_rank and not any(core in f for f in fwd):
         return
     S = T.sem
     ACT = ActivationFunctionType
     ALU = AluOpType
     AX = AxisListType.X
     V, A, PE = g.vector, g.scalar, g.tensor
-    cores = list(T.cores)
-    slot, on, off = _plan(cores, topo)
-    me = slot[core]
-    here = sorted(slot[d] for d in cores if topo.chip(d) == topo.chip(core))
-    n_on = sum(len(e) for c in cores if c != core for call in on[c] for ds, e in call if core in ds)
-    n_off = sum(len(e) for c in off for ds, e in off[c] if core in ds)
     NP = len(PARTS)
+    here = sorted(slot[d] for d in cores if topo.chip(d) == topo.chip(core))
+    n_on = [sum(len(e) for c in hop[p] for call in hop[p][c] for ds, e in call if core in ds) for p in range(NP)]
+    n_off = [sum(len(e) for c in fwd[p] for ds, e in fwd[p][c] if core in ds) for p in range(NP)]
+    n_idn = sum(len(e) for c in ident for ds, e in ident[c] if core in ds)
 
     def blk(b):
         return slice(b * P, (b + 1) * P)
 
-    def send(transfers, piece, sem):
+    def col(b):
+        return slice(b, b + 1)
+
+    def send(transfers, src, dst, sem):
         g.remote_dma_fused(
             [RemoteDMATransfer(dst_ids=[DstId(rid=topo.addr(d)[0], pnc=topo.addr(d)[1]) for d in ds],
-                               dma_engine_mask=_mask(e), remote_sem=sem, srcs=[piece], dsts=[piece for d in ds])
+                               dma_engine_mask=_mask(e), remote_sem=sem, srcs=[src], dsts=[dst for d in ds])
              for ds, e in transfers], local_sem=S.sent)
         return sum(len(e) for ds, e in transfers)
 
     def names(p):
         lo, hi = PARTS[p]
-        return (lo, hi, hi - lo, _width(hi - lo), T["G%d" % p],
-                lambda n: T["%s%d" % (n, p)], lambda n: S["%s%d" % (n, p)])
+        return lo, hi, hi - lo, _width(hi - lo), T["G%d" % p], lambda n: S["%s%d" % (n, p)]
+
+    def forwards():
+        n = 0
+        for p in range(NP):
+            if core in fwd[p]:
+                lo, hi, nb, W, G, s = names(p)
+                piece = G[:, here[0] * W:(here[-1] + 1) * W]
+                g.wait_ge(s("on"), n_on[p])
+                n += send(fwd[p][core], piece, piece, s("off"))
+        return n
+
+    if not is_rank:
+        V.memset(T.ones[:], 1.0).then_inc(S.c1, 1)
+        g.wait_ge(S.c1, 1)
+        g.affine_select(T.idn[:], T.ones[:], [[-1, P]], ALU.is_equal, 0.0, 0, 1).then_inc(S.c2, 1)
+        g.wait_ge(S.c2, 1)
+        sent = send(ident[core], T.idn[:], T.idn[:], S.c3)
+        sent += forwards()
+        g.wait_ge(S.sent, sent)
+        return
+
+    me = slot[core]
+
+    def own(p):
+        W = _width(PARTS[p][1] - PARTS[p][0])
+        return (T["own%d" % p], 0) if back[p] else (T["G%d" % p], me * W)
 
     for b in range(4):
         q = g.sync if b % 2 == 0 else g.scalar
@@ -121,14 +183,18 @@ def rank_program(g, core, T, topo):
     g.wait_ge(S.c1, 1)
     g.affine_select(T.idx[:, 0:P], T.ones[:], [[-1, P]], ALU.is_equal, -1.0 / 128.0, 0, 1).then_inc(S.c2, 1)
     for p in range(NP):
-        lo, hi, nb, W, G, t, s = names(p)
-        V.memset(G[:, me * W + 2 * nb:(me + 1) * W], 0.0).then_inc(s("pad"), 1)
-    V.wait_ge(S.c2, 2)
-    V.tensor_scalar(T.idn[:], T.idx[:, 0:P], 1.0 / 128.0, None, ALU.add).then_inc(S.c3, 1)
+        lo, hi, nb, W, G, s = names(p)
+        O, o = own(p)
+        V.memset(O[:, o + 2 * nb:o + W], 0.0).then_inc(s("pad"), 1)
+    if not n_idn:
+        V.wait_ge(S.c2, 2)
+        V.tensor_scalar(T.idn[:], T.idx[:, 0:P], 1.0 / 128.0, None, ALU.add).then_inc(S.c3, 1)
+        n_idn = 1
 
     PE.wait_ge(S.c2, 2)
     for p in range(NP):
-        lo, hi, nb, W, G, t, s = names(p)
+        lo, hi, nb, W, G, s = names(p)
+        O, o = own(p)
         for b in range(lo, hi):
             j = b - lo
             xT = T["xT%d" % b]
@@ -136,98 +202,126 @@ def rank_program(g, core, T, topo):
             PE.matmul(xT[:, 0:P + 1], T.xs[:, blk(b)], T.idx[:, 0:P + 1], True, True).then_inc(S["tr%d" % b], 1)
             A.wait_ge(S["tr%d" % b], 1)
             A.activation(T.junk[:, blk(b)], xT[:, 0:P], ACT.Square, scale=1.0 / 8.0,
-                         accum_out=G[:, me * W + nb + j:me * W + nb + j + 1]).then_inc(S["sq%d" % b], 1)
-            A.activation(G[:, me * W + j:me * W + j + 1], xT[:, P:P + 1], ACT.Copy).then_inc(S["ucp%d" % b], 1)
+                         accum_out=O[:, o + nb + j:o + nb + j + 1]).then_inc(S["sq%d" % b], 1)
+            A.activation(O[:, o + j:o + j + 1], xT[:, P:P + 1], ACT.Copy).then_inc(S["ucp%d" % b], 1)
 
     sent = 0
     for p in range(NP):
-        lo, hi, nb, W, G, t, s = names(p)
+        lo, hi, nb, W, G, s = names(p)
+        O, o = own(p)
         g.wait_ge(s("pad"), 1)
         for b in range(lo, hi):
             g.wait_ge(S["sq%d" % b], 1)
             g.wait_ge(S["ucp%d" % b], 1)
-        for call in on[core]:
-            sent += send(call, G[:, me * W:(me + 1) * W], s("on"))
-    if core in off:
-        for p in range(NP):
-            lo, hi, nb, W, G, t, s = names(p)
-            g.wait_ge(s("on"), n_on)
-            sent += send(off[core], G[:, here[0] * W:(here[-1] + 1) * W], s("off"))
+        for call in hop[p][core]:
+            sent += send(call, O[:, o:o + W], G[:, me * W:(me + 1) * W], s("on"))
+    sent += forwards()
     g.wait_ge(S.sent, sent)
 
+    for p in range(NP):
+        lo, hi, nb, W, G, s = names(p)
+        O, o = own(p)
+        for b in range(lo, hi):
+            A.wait_ge(S["sq%d" % b], 1)
+        A.activation(T.S8[:, lo:hi], O[:, o + nb:o + 2 * nb], ACT.Sqrt, bias=64.0 * EPS, scale=32.0).then_inc(S.hs, 1)
+    A.wait_ge(S.hs, NP)
+    A.wait_ge(S.c3, n_idn)
+    for b in range(4):
+        A.activation(T.dgs8[:, blk(b)], T.idn[:], ACT.Copy, scale=T.S8[:, col(b)]).then_inc(S.hd, 1)
+    V.wait_ge(S.hs, NP)
+    V.tensor_tensor(T.s2[:], T.S8[:], T.S8[:], ALU.mult).then_inc(S.h1, 1)
+    V.wait_ge(S.h1, 1)
+    V.reciprocal(T.rr[:], T.s2[:]).then_inc(S.h2, 1)
+    V.wait_ge(S.h2, 1)
+    V.tensor_scalar(T.k8[:], T.rr[:], 8.0, None, ALU.mult).then_inc(S.hk, 1)
+    V.tensor_scalar(T.k16[:], T.rr[:], 4.0, None, ALU.mult).then_inc(S.hk, 1)
+    V.tensor_scalar(T.ke[:], T.rr[:], 64.0 * EPS, None, ALU.mult).then_inc(S.hk, 1)
+    V.wait_ge(S.hk, 3)
+    A.wait_ge(S.hk, 3)
+    A.wait_ge(S.hd, 4)
+
     def arrived(q, p):
-        lo, hi, nb, W, G, t, s = names(p)
-        q.wait_ge(s("on"), n_on)
-        q.wait_ge(s("off"), n_off)
+        lo, hi, nb, W, G, s = names(p)
+        if n_on[p]:
+            q.wait_ge(s("on"), n_on[p])
+        q.wait_ge(s("off"), n_off[p])
         for b in range(lo, hi):
             q.wait_ge(S["ucp%d" % b], 1)
             q.wait_ge(S["sq%d" % b], 1)
 
-    def diags(p):
-        lo, hi, nb, W, G, t, s = names(p)
-        A.wait_ge(s("ssd"), 1)
+    def v_sums(p):
+        lo, hi, nb, W, G, s = names(p)
+        arrived(V, p)
         for b in range(lo, hi):
-            j = b - lo
-            A.activation(T.dg[:, blk(b)], T.idn[:], ACT.Copy, scale=t("sd")[:, j:j + 1]).then_inc(S["dgs%d" % b], 1)
+            V.tensor_reduce(T.NS[:, col(b)], G[:, b - lo:NR * W:W], AX, ALU.add, negate=True).then_inc(S["jns%d" % b], 1)
+        for b in range(lo, hi):
+            V.tensor_reduce(T.SQ[:, col(b)], G[:, nb + b - lo:NR * W:W], AX, ALU.add).then_inc(S["jsq%d" % b], 1)
 
-    lo, hi, nb, W0, G0, t0, s0 = names(0)
-    arrived(V, 0)
-    V.tensor_reduce(t0("NS")[:], G0[:, 0:NR * W0:W0], AX, ALU.add, negate=True).then_inc(s0("sns"), 1)
-    V.tensor_reduce(t0("SQ")[:], G0[:, 1:NR * W0:W0], AX, ALU.add).then_inc(s0("ssq"), 1)
-    V.wait_ge(s0("ssq"), 1)
-    V.tensor_scalar(t0("w")[:], t0("SQ")[:], 1.0 / 16.0, EPS, ALU.mult, ALU.add).then_inc(s0("sw"), 1)
-    V.wait_ge(s0("sns"), 1)
-    V.tensor_scalar(T.dm0[:], G0[:, me * W0:me * W0 + 1], 8.0, t0("NS")[:, 0:1], ALU.mult, ALU.add).then_inc(S.sdm0, 1)
-    arrived(A, 0)
-    A.wait_ge(s0("sns"), 1)
-    A.activation(t0("D")[:], G0[:, 0:NR * W0:W0], ACT.Square, bias=t0("NS")[:, 0:1], scale=8.0,
-                 accum_out=t0("E")[:, 0:1]).then_inc(s0("se"), 1)
-    A.wait_ge(s0("se"), 1)
-    A.wait_ge(s0("sw"), 1)
-    A.activation(t0("sd")[:], t0("E")[:], ACT.Sqrt, bias=t0("w")[:, 0:1], scale=0.125).then_inc(s0("ssd"), 1)
-    A.wait_ge(S.c3, 1)
-    diags(0)
+    def v_bias(p):
+        lo, hi, nb, W, G, s = names(p)
+        for b in range(lo, hi):
+            V.wait_ge(S["jsq%d" % b], 1)
+            V.tensor_scalar(T.wr[:, col(b)], T.SQ[:, col(b)], T.k16[:, col(b)], T.ke[:, col(b)],
+                            ALU.mult, ALU.add).then_inc(S["jwr%d" % b], 1)
+        V.tensor_scalar(T.w8[:, lo:hi], T.SQ[:, lo:hi], 0.5, 8.0 * EPS, ALU.mult, ALU.add).then_inc(s("sw"), 1)
 
-    lo, hi, nb, W, G, t, s = names(1)
-    X, D = t("X"), t("D")
-    arrived(V, 1)
-    for j in range(nb):
-        V.tensor_reduce(t("NS")[:, j:j + 1], G[:, j:NR * W:W], AX, ALU.add, negate=True).then_inc(S["jns%d" % j], 1)
-    for j in range(nb):
-        V.tensor_scalar(X[:, j * 16 + 8:j * 16 + 16], G[:, nb + j:NR * W:W], 0.5, EPS,
-                        ALU.mult, ALU.add).then_inc(s("sqp"), 1)
-    for j in range(nb):
-        V.wait_ge(S["jns%d" % j], 1)
-        V.tensor_scalar(D[:, j * NR:(j + 1) * NR], G[:, j:NR * W:W], 8.0, t("NS")[:, j:j + 1],
-                        ALU.mult, ALU.add).then_inc(S["jd%d" % j], 1)
-    V.wait_ge(s0("se"), 1)
-    V.wait_ge(s0("sw"), 1)
-    V.tensor_scalar(t0("v")[:], t0("E")[:], 0.125, t0("w")[:, 0:1], ALU.mult, ALU.add).then_inc(s0("sv"), 1)
-    for j in range(nb):
-        V.wait_ge(S["jd%d" % j], 1)
-        V.tensor_tensor(X[:, j * 16:j * 16 + 8], D[:, j * NR:(j + 1) * NR], D[:, j * NR:(j + 1) * NR],
-                        ALU.mult).then_inc(S["jd2%d" % j], 1)
-    V.wait_ge(s0("sv"), 1)
-    V.reciprocal(t0("r")[:], t0("v")[:]).then_inc(s0("sr"), 1)
-    V.wait_ge(s("sqp"), nb)
-    for j in range(nb):
-        V.wait_ge(S["jd2%d" % j], 1)
-        V.tensor_reduce(t("v")[:, j:j + 1], X[:, j * 16:(j + 1) * 16], AX, ALU.add).then_inc(S["jv%d" % j], 1)
-    V.wait_ge(s0("sr"), 1)
-    V.wait_ge(S.sdm0, 1)
-    V.tensor_scalar(T.zr[:, blk(0)], T.xT0[:, 0:P], T.dm0[:, 0:1], t0("r")[:, 0:1],
-                    ALU.subtract, ALU.mult).then_inc(S.ap0, 1)
-    for j in range(nb):
-        V.wait_ge(S["jv%d" % j], 1)
-        A.wait_ge(S["jv%d" % j], 1)
-    V.reciprocal(t("r")[:], t("v")[:]).then_inc(s("sr"), 1)
-    A.activation(t("sd")[:], t("v")[:], ACT.Sqrt, scale=8.0).then_inc(s("ssd"), 1)
-    diags(1)
-    V.wait_ge(s("sr"), 1)
-    for b in range(lo, hi):
-        j = b - lo
-        V.tensor_scalar(T.zr[:, blk(b)], T["xT%d" % b][:, 0:P], D[:, j * NR + me:j * NR + me + 1], t("r")[:, j:j + 1],
-                        ALU.subtract, ALU.mult).then_inc(S["ap%d" % b], 1)
+    def v_own(p):
+        lo, hi, nb, W, G, s = names(p)
+        for b in range(lo, hi):
+            V.wait_ge(S["jns%d" % b], 1)
+            V.tensor_scalar(T.dm[:, col(b)], G[:, me * W + b - lo:me * W + b - lo + 1], 8.0, T.NS[:, col(b)],
+                            ALU.mult, ALU.add).then_inc(S["jdm%d" % b], 1)
+
+    def v_var(p):
+        lo, hi, nb, W, G, s = names(p)
+        for b in range(lo, hi):
+            V.wait_ge(S["je%d" % b], 1)
+        V.wait_ge(s("sw"), 1)
+        V.tensor_tensor(T.v8[:, lo:hi], T.E[:, lo:hi], T.w8[:, lo:hi], ALU.add).then_inc(s("sv"), 1)
+
+    def v_rec(p):
+        lo, hi, nb, W, G, s = names(p)
+        V.wait_ge(s("sv"), 1)
+        V.reciprocal(T.r8[:, lo:hi], T.v8[:, lo:hi]).then_inc(s("sr"), 1)
+
+    def v_norm(p):
+        lo, hi, nb, W, G, s = names(p)
+        V.wait_ge(s("sr"), 1)
+        for b in range(lo, hi):
+            V.wait_ge(S["jdm%d" % b], 1)
+            V.tensor_scalar(T.zr[:, blk(b)], T["xT%d" % b][:, 0:P], T.dm[:, col(b)], T.r8[:, col(b)],
+                            ALU.subtract, ALU.mult).then_inc(S["ap%d" % b], 1)
+
+    def a_join(p):
+        lo, hi, nb, W, G, s = names(p)
+        arrived(A, p)
+        for b in range(lo, hi):
+            A.wait_ge(S["jns%d" % b], 1)
+            A.activation(T.Dj[:, b * NR:(b + 1) * NR], G[:, b - lo:NR * W:W], ACT.Square, bias=T.NS[:, col(b)], scale=8.0,
+                         accum_out=T.E[:, col(b)]).then_inc(S["je%d" % b], 1)
+        for b in range(lo, hi):
+            A.wait_ge(S["je%d" % b], 1)
+            A.wait_ge(S["jwr%d" % b], 1)
+            A.activation(T.tt[:, col(b)], T.E[:, col(b)], ACT.Sqrt, bias=T.wr[:, col(b)],
+                         scale=T.k8[:, col(b)]).then_inc(S["jt%d" % b], 1)
+        for b in range(lo, hi):
+            A.wait_ge(S["jt%d" % b], 1)
+            A.activation(T.dg[:, blk(b)], T.dgs8[:, blk(b)], ACT.Copy, scale=T.tt[:, col(b)]).then_inc(S["dgs%d" % b], 1)
+
+    v_sums(0)
+    v_bias(0)
+    v_own(0)
+    v_sums(1)
+    v_var(0)
+    v_bias(1)
+    v_rec(0)
+    v_own(1)
+    v_norm(0)
+    v_var(1)
+    v_rec(1)
+    v_norm(1)
+    a_join(0)
+    a_join(1)
 
     for b in range(4):
         PE.wait_ge(S["ap%d" % b], 1)

import numpy as np
from concourse.bass import DstId, RemoteDMATransfer
from concourse.mybir import dt, AluOpType, AxisListType, ActivationFunctionType

P = 128
NR = 8
SIM = 64
EPS = 0.01
PARTS = ((0, 1), (1, 4))


def _width(nb):
    return ((2 * nb + 3) // 4) * 4


SCRATCH = {
    "xs": ("sbuf", [P, 512], "float32"),
    "ones": ("sbuf", [P, P], "float32"),
    "idx": ("sbuf", [P, 132], "float32"),
    "idn": ("sbuf", [P, P], "float32"),
    "junk": ("sbuf", [P, 512], "float32"),
    "zr": ("sbuf", [P, 512], "float32"),
    "dgs8": ("sbuf", [P, 512], "float32"),
    "dg": ("sbuf", [P, 512], "float32"),
    "ys": ("sbuf", [P, 512], "float32"),
    "Dj": ("sbuf", [P, 4 * NR], "float32"),
}
for _n in ("NS", "SQ", "wr", "w8", "E", "v8", "r8", "tt", "dm", "S8", "s2", "rr", "k8", "k16", "ke"):
    SCRATCH[_n] = ("sbuf", [P, 4], "float32")
SEMAPHORES = ["c1", "c2", "c3", "sent", "hs", "h1", "h2", "hk", "hd"]
for _b in range(4):
    SCRATCH["xT%d" % _b] = ("psum", [P, 512], "float32")
    SCRATCH["yo%d" % _b] = ("psum", [P, 512], "float32")
    SEMAPHORES += [n + str(_b) for n in ("ld", "tr", "ucp", "sq", "ap", "dgs", "bt", "cp", "st",
                                         "jns", "jsq", "jwr", "jdm", "je", "jt")]
for _p, (_lo, _hi) in enumerate(PARTS):
    _nb = _hi - _lo
    SCRATCH["G%d" % _p] = ("sbuf", [P, NR * _width(_nb)], "float32")
    SCRATCH["own%d" % _p] = ("sbuf", [P, _width(_nb)], "float32")
    SEMAPHORES += [n + str(_p) for n in ("pad", "on", "off", "sw", "sv", "sr")]


def _bits(mask):
    return [e for e in range(mask.bit_length()) if (mask >> e) & 1]


def _mask(engines):
    return sum(1 << e for e in engines)


def _pow2(n):
    k = 1
    while k * 2 <= n:
        k *= 2
    return k


def _deal(dests, engines):
    if not dests:
        return []
    k = _pow2(len(engines) // len(dests))
    return [([d], engines[i * k:(i + 1) * k]) for i, d in enumerate(dests)]


def _pick(pool, load, d, topo):
    same = [f for f in pool if topo.die(f) == topo.die(d)] or pool
    return min(same, key=lambda f: (len(load[f]), pool.index(f)))


def _plan(cores, topo):
    order = sorted(cores, key=lambda c: (topo.chip(c), cores.index(c)))
    slot = {c: i for i, c in enumerate(order)}
    hop = [{} for p in PARTS]
    fwd = [{} for p in PARTS]
    back = [False for p in PARTS]
    ident = {}
    for ch in sorted(set(topo.chip(c) for c in cores)):
        here = [c for c in cores if topo.chip(c) == ch]
        there = [c for c in cores if topo.chip(c) != ch]
        able = [c for c in range(SIM) if topo.chip(c) == ch and all(topo.may_write(c, d) for d in there)]
        relays = [c for c in able if c in here]
        helpers = [c for c in able if c not in here]

        def engines(c):
            peer = [d for d in here if d != c][0]
            out = _bits(topo.mask(c, there[0]))
            return out, [e for e in _bits(topo.mask(c, peer)) if e not in out]

        for p in range(len(PARTS)):
            back[p] = p == 0 and len(helpers) > 0
            fw = helpers if back[p] else relays
            far = {f: [] for f in fw}
            near = {f: [] for f in fw}
            for d in there:
                far[_pick(fw, far, d, topo)].append(d)
            for d in here:
                if back[p]:
                    near[_pick(fw, near, d, topo)].append(d)
            for c in here:
                out, others = engines(c)
                hop[p][c] = [_deal([f for f in fw if f != c], out)]
                rest = [d for d in here if d != c and d not in fw]
                if rest and not back[p]:
                    hop[p][c].append([(rest, others[:_pow2(len(others))])])
            for f in fw:
                out, others = engines(f)
                fwd[p][f] = _deal(far[f], out) + _deal(near[f], others)
        give = {f: [] for f in helpers}
        for d in here:
            if helpers:
                give[_pick(helpers, give, d, topo)].append(d)
        for f in helpers:
            out, others = engines(f)
            ident[f] = _deal(give[f], out + others)
    return slot, hop, fwd, back, ident


def rank_program(g, core, T, topo):
    cores = list(T.cores)
    slot, hop, fwd, back, ident = _plan(cores, topo)
    is_rank = T.rank_of(core) is not None
    if not is_rank and not any(core in f for f in fwd):
        return
    S = T.sem
    ACT = ActivationFunctionType
    ALU = AluOpType
    AX = AxisListType.X
    V, A, PE = g.vector, g.scalar, g.tensor
    NP = len(PARTS)
    here = sorted(slot[d] for d in cores if topo.chip(d) == topo.chip(core))
    n_on = [sum(len(e) for c in hop[p] for call in hop[p][c] for ds, e in call if core in ds) for p in range(NP)]
    n_off = [sum(len(e) for c in fwd[p] for ds, e in fwd[p][c] if core in ds) for p in range(NP)]
    n_idn = sum(len(e) for c in ident for ds, e in ident[c] if core in ds)

    def blk(b):
        return slice(b * P, (b + 1) * P)

    def col(b):
        return slice(b, b + 1)

    def send(transfers, src, dst, sem):
        g.remote_dma_fused(
            [RemoteDMATransfer(dst_ids=[DstId(rid=topo.addr(d)[0], pnc=topo.addr(d)[1]) for d in ds],
                               dma_engine_mask=_mask(e), remote_sem=sem, srcs=[src], dsts=[dst for d in ds])
             for ds, e in transfers], local_sem=S.sent)
        return sum(len(e) for ds, e in transfers)

    def names(p):
        lo, hi = PARTS[p]
        return lo, hi, hi - lo, _width(hi - lo), T["G%d" % p], lambda n: S["%s%d" % (n, p)]

    def forwards():
        n = 0
        for p in range(NP):
            if core in fwd[p]:
                lo, hi, nb, W, G, s = names(p)
                piece = G[:, here[0] * W:(here[-1] + 1) * W]
                g.wait_ge(s("on"), n_on[p])
                n += send(fwd[p][core], piece, piece, s("off"))
        return n

    if not is_rank:
        V.memset(T.ones[:], 1.0).then_inc(S.c1, 1)
        g.wait_ge(S.c1, 1)
        g.affine_select(T.idn[:], T.ones[:], [[-1, P]], ALU.is_equal, 0.0, 0, 1).then_inc(S.c2, 1)
        g.wait_ge(S.c2, 1)
        sent = send(ident[core], T.idn[:], T.idn[:], S.c3)
        sent += forwards()
        g.wait_ge(S.sent, sent)
        return

    me = slot[core]

    def own(p):
        W = _width(PARTS[p][1] - PARTS[p][0])
        return (T["own%d" % p], 0) if back[p] else (T["G%d" % p], me * W)

    for b in range(4):
        q = g.sync if b % 2 == 0 else g.scalar
        q.dma_start(T.xs[:, blk(b)], T.x[:, blk(b)]).then_inc(S["ld%d" % b], 16)
    V.memset(T.ones[:], 1.0 - 1.0 / 128.0).then_inc(S.c1, 1)
    V.memset(T.idx[:, P:P + 1], -1.0 / 1024.0).then_inc(S.c2, 1)
    g.wait_ge(S.c1, 1)
    g.affine_select(T.idx[:, 0:P], T.ones[:], [[-1, P]], ALU.is_equal, -1.0 / 128.0, 0, 1).then_inc(S.c2, 1)
    for p in range(NP):
        lo, hi, nb, W, G, s = names(p)
        O, o = own(p)
        V.memset(O[:, o + 2 * nb:o + W], 0.0).then_inc(s("pad"), 1)
    if not n_idn:
        V.wait_ge(S.c2, 2)
        V.tensor_scalar(T.idn[:], T.idx[:, 0:P], 1.0 / 128.0, None, ALU.add).then_inc(S.c3, 1)
        n_idn = 1

    PE.wait_ge(S.c2, 2)
    for p in range(NP):
        lo, hi, nb, W, G, s = names(p)
        O, o = own(p)
        for b in range(lo, hi):
            j = b - lo
            xT = T["xT%d" % b]
            PE.wait_ge(S["ld%d" % b], 16)
            PE.matmul(xT[:, 0:P + 1], T.xs[:, blk(b)], T.idx[:, 0:P + 1], True, True).then_inc(S["tr%d" % b], 1)
            A.wait_ge(S["tr%d" % b], 1)
            A.activation(T.junk[:, blk(b)], xT[:, 0:P], ACT.Square, scale=1.0 / 8.0,
                         accum_out=O[:, o + nb + j:o + nb + j + 1]).then_inc(S["sq%d" % b], 1)
            A.activation(O[:, o + j:o + j + 1], xT[:, P:P + 1], ACT.Copy).then_inc(S["ucp%d" % b], 1)

    sent = 0
    for p in range(NP):
        lo, hi, nb, W, G, s = names(p)
        O, o = own(p)
        g.wait_ge(s("pad"), 1)
        for b in range(lo, hi):
            g.wait_ge(S["sq%d" % b], 1)
            g.wait_ge(S["ucp%d" % b], 1)
        for call in hop[p][core]:
            sent += send(call, O[:, o:o + W], G[:, me * W:(me + 1) * W], s("on"))
    sent += forwards()
    g.wait_ge(S.sent, sent)

    for p in range(NP):
        lo, hi, nb, W, G, s = names(p)
        O, o = own(p)
        for b in range(lo, hi):
            A.wait_ge(S["sq%d" % b], 1)
        A.activation(T.S8[:, lo:hi], O[:, o + nb:o + 2 * nb], ACT.Sqrt, bias=64.0 * EPS, scale=32.0).then_inc(S.hs, 1)
    A.wait_ge(S.hs, NP)
    A.wait_ge(S.c3, n_idn)
    for b in range(4):
        A.activation(T.dgs8[:, blk(b)], T.idn[:], ACT.Copy, scale=T.S8[:, col(b)]).then_inc(S.hd, 1)
    V.wait_ge(S.hs, NP)
    V.tensor_tensor(T.s2[:], T.S8[:], T.S8[:], ALU.mult).then_inc(S.h1, 1)
    V.wait_ge(S.h1, 1)
    V.reciprocal(T.rr[:], T.s2[:]).then_inc(S.h2, 1)
    V.wait_ge(S.h2, 1)
    V.tensor_scalar(T.k8[:], T.rr[:], 8.0, None, ALU.mult).then_inc(S.hk, 1)
    V.tensor_scalar(T.k16[:], T.rr[:], 4.0, None, ALU.mult).then_inc(S.hk, 1)
    V.tensor_scalar(T.ke[:], T.rr[:], 64.0 * EPS, None, ALU.mult).then_inc(S.hk, 1)
    V.wait_ge(S.hk, 3)
    A.wait_ge(S.hk, 3)
    A.wait_ge(S.hd, 4)

    def arrived(q, p):
        lo, hi, nb, W, G, s = names(p)
        if n_on[p]:
            q.wait_ge(s("on"), n_on[p])
        q.wait_ge(s("off"), n_off[p])
        for b in range(lo, hi):
            q.wait_ge(S["ucp%d" % b], 1)
            q.wait_ge(S["sq%d" % b], 1)

    def v_sums(p):
        lo, hi, nb, W, G, s = names(p)
        arrived(V, p)
        for b in range(lo, hi):
            V.tensor_reduce(T.NS[:, col(b)], G[:, b - lo:NR * W:W], AX, ALU.add, negate=True).then_inc(S["jns%d" % b], 1)
        for b in range(lo, hi):
            V.tensor_reduce(T.SQ[:, col(b)], G[:, nb + b - lo:NR * W:W], AX, ALU.add).then_inc(S["jsq%d" % b], 1)

    def v_bias(p):
        lo, hi, nb, W, G, s = names(p)
        for b in range(lo, hi):
            V.wait_ge(S["jsq%d" % b], 1)
            V.tensor_scalar(T.wr[:, col(b)], T.SQ[:, col(b)], T.k16[:, col(b)], T.ke[:, col(b)],
                            ALU.mult, ALU.add).then_inc(S["jwr%d" % b], 1)
        V.tensor_scalar(T.w8[:, lo:hi], T.SQ[:, lo:hi], 0.5, 8.0 * EPS, ALU.mult, ALU.add).then_inc(s("sw"), 1)

    def v_own(p):
        lo, hi, nb, W, G, s = names(p)
        for b in range(lo, hi):
            V.wait_ge(S["jns%d" % b], 1)
            V.tensor_scalar(T.dm[:, col(b)], G[:, me * W + b - lo:me * W + b - lo + 1], 8.0, T.NS[:, col(b)],
                            ALU.mult, ALU.add).then_inc(S["jdm%d" % b], 1)

    def v_var(p):
        lo, hi, nb, W, G, s = names(p)
        for b in range(lo, hi):
            V.wait_ge(S["je%d" % b], 1)
        V.wait_ge(s("sw"), 1)
        V.tensor_tensor(T.v8[:, lo:hi], T.E[:, lo:hi], T.w8[:, lo:hi], ALU.add).then_inc(s("sv"), 1)

    def v_rec(p):
        lo, hi, nb, W, G, s = names(p)
        V.wait_ge(s("sv"), 1)
        V.reciprocal(T.r8[:, lo:hi], T.v8[:, lo:hi]).then_inc(s("sr"), 1)

    def v_norm(p):
        lo, hi, nb, W, G, s = names(p)
        V.wait_ge(s("sr"), 1)
        for b in range(lo, hi):
            V.wait_ge(S["jdm%d" % b], 1)
            V.tensor_scalar(T.zr[:, blk(b)], T["xT%d" % b][:, 0:P], T.dm[:, col(b)], T.r8[:, col(b)],
                            ALU.subtract, ALU.mult).then_inc(S["ap%d" % b], 1)

    def a_join(p):
        lo, hi, nb, W, G, s = names(p)
        arrived(A, p)
        for b in range(lo, hi):
            A.wait_ge(S["jns%d" % b], 1)
            A.activation(T.Dj[:, b * NR:(b + 1) * NR], G[:, b - lo:NR * W:W], ACT.Square, bias=T.NS[:, col(b)], scale=8.0,
                         accum_out=T.E[:, col(b)]).then_inc(S["je%d" % b], 1)
        for b in range(lo, hi):
            A.wait_ge(S["je%d" % b], 1)
            A.wait_ge(S["jwr%d" % b], 1)
            A.activation(T.tt[:, col(b)], T.E[:, col(b)], ACT.Sqrt, bias=T.wr[:, col(b)],
                         scale=T.k8[:, col(b)]).then_inc(S["jt%d" % b], 1)
        for b in range(lo, hi):
            A.wait_ge(S["jt%d" % b], 1)
            A.activation(T.dg[:, blk(b)], T.dgs8[:, blk(b)], ACT.Copy, scale=T.tt[:, col(b)]).then_inc(S["dgs%d" % b], 1)

    v_sums(0)
    v_bias(0)
    v_own(0)
    v_sums(1)
    v_var(0)
    v_bias(1)
    v_rec(0)
    v_own(1)
    v_norm(0)
    v_var(1)
    v_rec(1)
    v_norm(1)
    a_join(0)
    a_join(1)

    for b in range(4):
        PE.wait_ge(S["ap%d" % b], 1)
        PE.wait_ge(S["dgs%d" % b], 1)
        PE.matmul(T["yo%d" % b][:, 0:P], T.zr[:, blk(b)], T.dg[:, blk(b)], True, True).then_inc(S["bt%d" % b], 1)
    for b in range(4):
        if b % 2 == 0:
            A.wait_ge(S["bt%d" % b], 1)
            A.activation(T.ys[:, blk(b)], T["yo%d" % b][:, 0:P], ACT.Copy).then_inc(S["cp%d" % b], 1)
        else:
            V.wait_ge(S["bt%d" % b], 1)
            V.tensor_copy(T.ys[:, blk(b)], T["yo%d" % b][:, 0:P]).then_inc(S["cp%d" % b], 1)
        g.sync.wait_ge(S["cp%d" % b], 1)
        g.sync.dma_start(T.y[:, blk(b)], T.ys[:, blk(b)]).then_inc(S["st%d" % b], 16)
    for b in range(4):
        g.sync.wait_ge(S["st%d" % b], 16)
